import numpy as np
import ml_dtypes


def mxq(x, axis, fmt="e4m3"):
    dtype, down = {"e4m3": (ml_dtypes.float8_e4m3fn, 7), "e5m2": (ml_dtypes.float8_e5m2, 14)}[fmt]
    v = np.moveaxis(np.asarray(x, np.float32).astype(ml_dtypes.bfloat16).astype(np.float64), axis, -1)
    blocks = v.reshape(v.shape[:-1] + (-1, 32))
    amax = np.abs(blocks).max(-1, keepdims=True)
    byte = np.maximum(np.where(amax > 0, np.frexp(amax)[1] - 1 + 127, 0) - down, 1)
    scale = np.exp2(byte - 127.0)
    codes = (blocks / scale).astype(np.float32).astype(dtype).astype(np.float64)
    return np.moveaxis((codes * scale).reshape(v.shape), -1, axis)


WIDE = False


def mx_kscale(k):
    if not WIDE:
        return np.ones(k)
    levels = np.array([10, -10, 5, -5, 0])
    if k % 512:
        return np.exp2(np.random.permutation(np.resize(levels, k // 32))).repeat(32)
    a = np.empty((k // 512, 16))
    for p in range(k // 512):
        a[p, :8] = np.random.permutation(np.resize(levels, 8))
        for g in range(8):
            far = levels[np.abs(levels - a[p, g]) >= 10]
            a[p, g + 8] = far[np.random.randint(len(far))]
    return np.exp2(a.ravel()).repeat(32)


def f64(x):
    return np.asarray(x).astype(np.float64)


def striped(idx):
    return np.tile(idx.reshape(-1, 16).T, (8, 1)).astype(np.uint16)


def unstriped(offs):
    return offs[:16].T.reshape(-1).astype(np.int64)


def pack_weight(w):
    k, n = w.shape
    w = f64(np.asarray(w, np.float32).astype(ml_dtypes.bfloat16)).reshape(k // 32, 32, n)
    amax = np.abs(w).max(1)
    byte = np.clip(np.where(amax > 0, np.frexp(amax)[1] - 1 + 127 - 7, 1), 1, 254)
    scaled = (w * np.exp2(127.0 - byte)[:, None, :]).reshape(k, n).astype(np.float32)
    words = np.ascontiguousarray(scaled.reshape(k // 512, 128, 4, n).transpose(0, 1, 3, 2)).astype(ml_dtypes.float8_e4m3fn).view(np.uint8)
    return words, np.ascontiguousarray(byte.astype(np.uint8).reshape(k // 512, 16, n))


def unpack_weight(words, scales):
    g, p, n, _ = words.shape
    vals = np.ascontiguousarray(words).view(ml_dtypes.float8_e4m3fn).astype(np.float64) * np.repeat(np.exp2(scales.astype(np.float64) - 127.0), 8, axis=1)[..., None]
    return vals.transpose(0, 1, 3, 2).reshape(g * 512, n)


def sigmoid(v):
    return 1.0 / (1.0 + np.exp(-np.maximum(v, -700.0)))


K, T, S, H, W, C, U = 512, 2048, 256, 512, 128, 512, 512


def setup_inputs():
    n = np.random.standard_normal
    s = mx_kscale(K)[:, None]
    packed_xT = pack_weight(n((K, T)) * s)
    perm = np.random.permutation(U)
    return {
        "x_words": packed_xT[0],
        "x_scales": packed_xT[1],
        "w1": (n((K, H)) / np.sqrt(2 * K) / s).astype(np.float32),
        "w2": (n((K, H)) / np.sqrt(2 * K) / s).astype(np.float32),
        "gs": (np.random.uniform(0.5, 1.5, (K, 1)) / s).astype(np.float32),
        "sl": np.random.uniform(1.0, 2.0, (C, 1)).astype(np.float32),
        "th": (0.5 * n((C, 1))).astype(np.float32),
        "offs": striped(np.random.permutation(T)[:S]),
        "two": striped(np.random.permutation(T)[:S]),
        "n1": striped(np.random.permutation(S)[:W]),
        "n2": striped(np.random.permutation(S)[:W]),
        "n3": striped(np.random.permutation(S)),
        "cand": striped(np.random.permutation(T)[:C]),
        "n4": striped(perm[:S]),
        "n5": striped(perm[S:]),
        "n6": striped(np.random.permutation(S)),
    }


def reference(x_words, x_scales, w1, w2, gs, sl, th, offs, two, n1, n2, n3, cand, n4, n5, n6):
    x_cand = unpack_weight(x_words, x_scales)[:, unstriped(cand)]
    xq = unpack_weight(x_words, x_scales)[:, unstriped(offs)]
    x_two = unpack_weight(x_words, x_scales)[:, unstriped(two)]
    y = mxq(f64(w1), 0, "e4m3").T @ xq + mxq(f64(w2), 0, "e4m3").T @ x_two
    pa = y[:, unstriped(n2)]
    ds = y.copy()
    ds[:, unstriped(n1)] = pa
    z = f64(gs) * (ds - (0.5 * ds[:, unstriped(n3)]))
    s = 0.0625 * ((x_cand.T @ mxq(z, 0, "e4m3")))
    sg = sigmoid(f64(sl) * (s[:, unstriped(n6)] - f64(th)))
    st = s * sg
    ph = np.zeros((C, U))
    ph[:, unstriped(n4)] = s
    out = ph.copy()
    out[:, unstriped(n5)] = st
    return out

@@ -1,0 +1,185 @@
+from contextlib import ExitStack
+
+import concourse.mybir as mybir
+
+F32 = mybir.dt.float32
+BF16 = mybir.dt.bfloat16
+I32 = mybir.dt.int32
+U32 = mybir.dt.uint32
+U16 = mybir.dt.uint16
+U8 = mybir.dt.uint8
+FP8X4 = mybir.dt.float8_e4m3fn_x4
+ACT = mybir.ActivationFunctionType
+ALU = mybir.AluOpType
+
+P = 128
+PACK = 4
+K, T, S, H, W, C, U = 512, 2048, 256, 512, 128, 512, 512
+LANES = 16
+HEAD = 64
+PIECES = ((0, HEAD), (HEAD, 2 * HEAD), (2 * HEAD, S))
+
+FLOPS = 2 * K * H * S * 2 + 2 * H * C * S
+
+
+def entries(lst, lo, hi):
+    return lst[:, lo // LANES : hi // LANES]
+
+
+def tile_picked_dttzcksetepag_none_p_kernel(
+    tc, x_words, x_scales, w1, w2, gs, sl, th, offs, two, n1, n2, n3, cand, n4, n5, n6, out
+):
+    nc = tc.nc
+    with ExitStack() as ctx:
+        lists = ctx.enter_context(tc.tile_pool(name="lists", bufs=1))
+        keep = ctx.enter_context(tc.tile_pool(name="keep", bufs=1))
+        psum = ctx.enter_context(tc.psum_pool(name="psum", bufs=1))
+
+        def load_list(name, src):
+            tile = lists.tile(list(src.shape), U16, name=name)
+            nc.sync.dma_start(tile[:], src)
+            return tile
+
+        def load_weight(name, src):
+            raw = keep.tile([P, PACK, H], F32, name=name)
+            nc.sync.dma_start(out=raw[:], in_=src.rearrange("(p j) c -> p j c", j=PACK))
+            return raw
+
+        w1_raw = load_weight("w1_raw", w1)
+        scale_rows = keep.tile([P, T // 4], I32, name="scale_rows")
+        for q in range(4):
+            nc.scalar.dma_start(out=scale_rows[32 * q : 32 * q + 4, :], in_=x_scales[0][4 * q : 4 * q + 4, :].bitcast(I32))
+        offs_l = load_list("offs_l", offs)
+        two_l = load_list("two_l", two)
+        w2_raw = load_weight("w2_raw", w2)
+        xw = keep.tile([P, T], U32, name="xw")
+        nc.sync.dma_start(out=xw[:].bitcast(I32), in_=x_words[0].rearrange("p n t -> p (n t)").bitcast(I32))
+        gs_t = keep.tile([P, PACK], F32, name="gs_t")
+        nc.sync.dma_start(out=gs_t[:], in_=gs.rearrange("(p t) o -> p (t o)", t=PACK))
+        n2_l = load_list("n2_l", n2)
+        n1_l = load_list("n1_l", n1)
+        n3_l = load_list("n3_l", n3)
+        cand_l = load_list("cand_l", cand)
+        n4_l = load_list("n4_l", n4)
+        n6_l = load_list("n6_l", n6)
+        n5_l = load_list("n5_l", n5)
+        sl_t = keep.tile([P, 4], F32, name="sl_t")
+        th_t = keep.tile([P, 4], F32, name="th_t")
+        with nc.allow_non_contiguous_dma(reason="one value a partition and row tile"):
+            nc.sync.dma_start(out=sl_t[:], in_=sl.rearrange("(c p) o -> p (c o)", p=P))
+            nc.sync.dma_start(out=th_t[:], in_=th.rearrange("(c p) o -> p (c o)", p=P))
+
+        xs = keep.tile([P, T], U8, name="xs")
+        nc.vector.memset(xs[:].bitcast(I32), 0)
+        for q in range(4):
+            rows = slice(32 * q, 32 * q + 4)
+            nc.vector.tensor_copy(out=xs[rows, :].bitcast(I32), in_=scale_rows[rows, :])
+
+        def quantize_weight(name, raw):
+            grouped = keep.tile([P, PACK, P, PACK], BF16, name=name + "_grouped", align_bytes=64)
+            dst = grouped[:].rearrange("p t m j -> p m j t")
+            src = raw[:].rearrange("p j (m t) -> p m j t", t=PACK)
+            nc.vector.tensor_copy(out=dst[:, : P // 2], in_=src[:, : P // 2])
+            nc.scalar.copy(out=dst[:, P // 2 :], in_=src[:, P // 2 :])
+            return grouped
+
+        def quantize(name, grouped, width):
+            codes = keep.tile([P, width], U32, name=name + "_codes", align_bytes=64)
+            scales = keep.tile([P, width], U8, name=name + "_scales", align_bytes=64)
+            nc.vector.quantize_mx(out=codes[:].bitcast(FP8X4), scales=scales[:], in_=grouped)
+            return codes, scales
+
+        def gather(name, dtype, window, lst, n, tag=None):
+            got = keep.tile([P, n], dtype, name=name, tag=tag or name, align_bytes=64)
+            nc.vector.tensor_copy(out=got[:], in_=window[:].indirect(lst[:]))
+            return got
+
+        w1_g = quantize_weight("w1", w1_raw)
+        xq_s = gather("xq_s", U8, xs, offs_l, S)
+        w1_c, w1_s = quantize("w1", w1_g[:].rearrange("p t m j -> p (t m j)"), H)
+        two_s = gather("two_s", U8, xs, two_l, S)
+        w2_g = quantize_weight("w2", w2_raw)
+        w2_c, w2_s = quantize("w2", w2_g[:].rearrange("p t m j -> p (t m j)"), H)
+        xq_w = gather("xq_w", U32, xw, offs_l, S, tag="first_words")
+        two_w = gather("two_w", U32, xw, two_l, S, tag="second_words")
+
+        y_ps = [psum.tile([P, S], F32, name="y_ps%d" % t, tag="bank%d" % t) for t in range(PACK)]
+        for t in range(PACK):
+            cols = slice(t * P, (t + 1) * P)
+            nc.tensor.matmul_mx(out=y_ps[t][:], lhsT=w1_c[:, cols].bitcast(FP8X4), lhsT_scale=w1_s[:, cols],
+                                rhs=xq_w[:].bitcast(FP8X4), rhs_scale=xq_s[:], start=True, stop=False)
+        for t in range(PACK):
+            cols = slice(t * P, (t + 1) * P)
+            nc.tensor.matmul_mx(out=y_ps[t][:], lhsT=w2_c[:, cols].bitcast(FP8X4), lhsT_scale=w2_s[:, cols],
+                                rhs=two_w[:].bitcast(FP8X4), rhs_scale=two_s[:], start=False, stop=True)
+
+        ds = [keep.tile([P, S], F32, name="ds%d" % t) for t in range(PACK)]
+        for t in range(PACK):
+            nc.vector.tensor_scalar(out=ds[t][:], in0=y_ps[t][:], scalar1=gs_t[:, t : t + 1], scalar2=None, op0=ALU.mult)
+
+        cand_w = gather("cand_w", U32, xw, cand_l, C, tag="second_words")
+        cand_s = gather("cand_s", U8, xs, cand_l, C, tag="first_words")
+        bias = keep.tile([P, 4], F32, name="bias")
+        nc.vector.scalar_tensor_tensor(out=bias[:], in0=sl_t[:], scalar=-1.0, in1=th_t[:], op0=ALU.mult, op1=ALU.mult)
+
+        far_head = keep.tile([P, PACK, HEAD], F32, name="far_head")
+        for pair in range(PACK // 2):
+            pa = keep.tile([P, 2, W], F32, name="pa%d" % pair, tag="pa%d" % pair)
+            for u in range(2):
+                nc.scalar.activation(pa[:, u, :], ds[2 * pair + u][:].indirect(n2_l[:]), ACT.Copy)
+            for u in range(2):
+                nc.scalar.activation(ds[2 * pair + u][:].indirect(n1_l[:]), pa[:, u, :], ACT.Copy)
+            for u in range(2):
+                t = 2 * pair + u
+                nc.scalar.activation(far_head[:, t, :], ds[t][:].indirect(entries(n3_l, 0, HEAD)), ACT.Copy)
+        far_rest = keep.tile([P, PACK, S - HEAD], F32, name="far_rest", tag="pa1")
+        for lo, hi in PIECES[1:]:
+            for t in range(PACK):
+                nc.scalar.activation(far_rest[:, t, lo - HEAD : hi - HEAD], ds[t][:].indirect(entries(n3_l, lo, hi)), ACT.Copy)
+
+        z_codes = keep.tile([P, S], U32, name="z_codes", align_bytes=64)
+        z_scales = keep.tile([P, S], U8, name="z_scales", align_bytes=64)
+
+        def make_z(lo, hi):
+            n = hi - lo
+            planes = keep.tile([P, PACK, n], BF16, name="z_planes%d" % lo)
+            for t in range(PACK):
+                far = far_head[:, t, :] if lo == 0 else far_rest[:, t, lo - HEAD : hi - HEAD]
+                nc.vector.scalar_tensor_tensor(out=planes[:, t, :], in0=far, scalar=-0.5, in1=ds[t][:, lo:hi],
+                                               op0=ALU.mult, op1=ALU.add)
+            grouped = keep.tile([P, n, PACK], BF16, name="z_grouped%d" % lo, align_bytes=64)
+            nc.vector.tensor_copy(out=grouped[:].rearrange("p (c i) t -> p c t i", i=4),
+                                  in_=planes[:].rearrange("p t (c i) -> p c t i", i=4))
+            nc.vector.quantize_mx(out=z_codes[:, lo:hi].bitcast(FP8X4), scales=z_scales[:, lo:hi],
+                                  in_=grouped[:].rearrange("p n t -> p (n t)"))
+
+        s = [keep.tile([P, S], F32, name="s%d" % c) for c in range(4)]
+        page = [keep.tile([P, U], F32, name="page%d" % c) for c in range(4)]
+
+        def score(c, lo, hi, bank):
+            acc = psum.tile([P, hi - lo], F32, name="s_ps%d_%d" % (c, lo), tag="bank%d" % bank)
+            rows = slice(c * P, (c + 1) * P)
+            nc.tensor.matmul_mx(out=acc[:], lhsT=cand_w[:, rows].bitcast(FP8X4), lhsT_scale=cand_s[:, rows],
+                                rhs=z_codes[:, lo:hi].bitcast(FP8X4), rhs_scale=z_scales[:, lo:hi], start=True, stop=True)
+            nc.vector.tensor_scalar(out=s[c][:, lo:hi], in0=acc[:], scalar1=0.0625, scalar2=None, op0=ALU.mult)
+
+        for i, (lo, hi) in enumerate(PIECES):
+            make_z(lo, hi)
+            for c in range(4):
+                score(c, lo, hi, 4 * ((i + 1) % 2) + c)
+        for lo, hi in PIECES[:-1]:
+            for c in range(4):
+                nc.scalar.activation(page[c][:].indirect(entries(n4_l, lo, hi)), s[c][:, lo:hi], ACT.Copy)
+
+        last = PIECES[-1][0]
+        for c in range(4):
+            sg = keep.tile([P, S], F32, name="sg%d" % c)
+            for lo in range(0, S, S // 2):
+                hi = lo + S // 2
+                nc.scalar.activation(sg[:, lo:hi], s[c][:].indirect(entries(n6_l, lo, hi)), ACT.Sigmoid,
+                                     bias=bias[:, c : c + 1], scale=sl_t[:, c : c + 1])
+            st = keep.tile([P, S], F32, name="st%d" % c)
+            nc.vector.tensor_tensor(out=st[:], in0=s[c][:], in1=sg[:], op=ALU.mult)
+            nc.scalar.activation(page[c][:].indirect(entries(n4_l, last, S)), s[c][:, last:], ACT.Copy)
+            nc.scalar.activation(page[c][:].indirect(n5_l[:]), st[:], ACT.Copy)
+            nc.sync.dma_start(out=out[c * P : (c + 1) * P, :], in_=page[c][:])

@@ -16,8 +16,8 @@ P = 128
 PACK = 4
 K, T, S, H, W, C, U = 512, 2048, 256, 512, 128, 512, 512
 LANES = 16
-HEAD = 64
-PIECES = ((0, HEAD), (HEAD, 2 * HEAD), (2 * HEAD, S))
+HALF = S // 2
+QUARTER = S // 4
 
 FLOPS = 2 * K * H * S * 2 + 2 * H * C * S
 
@@ -45,19 +45,20 @@ def tile_picked_dttzcksetepag_none_p_kernel(
             nc.sync.dma_start(out=raw[:], in_=src.rearrange("(p j) c -> p j c", j=PACK))
             return raw
 
-        w1_raw = load_weight("w1_raw", w1)
-        scale_rows = keep.tile([P, T // 4], I32, name="scale_rows")
+        xs = keep.tile([P, T], U8, name="xs")
+        nc.vector.memset(xs[:].bitcast(I32), 0)
         for q in range(4):
-            nc.scalar.dma_start(out=scale_rows[32 * q : 32 * q + 4, :], in_=x_scales[0][4 * q : 4 * q + 4, :].bitcast(I32))
+            nc.scalar.dma_start(out=xs[32 * q : 32 * q + 4, :].bitcast(I32), in_=x_scales[0][4 * q : 4 * q + 4, :].bitcast(I32))
         offs_l = load_list("offs_l", offs)
         two_l = load_list("two_l", two)
+        n2_l = load_list("n2_l", n2)
+        n1_l = load_list("n1_l", n1)
+        w1_raw = load_weight("w1_raw", w1)
         w2_raw = load_weight("w2_raw", w2)
         xw = keep.tile([P, T], U32, name="xw")
         nc.sync.dma_start(out=xw[:].bitcast(I32), in_=x_words[0].rearrange("p n t -> p (n t)").bitcast(I32))
         gs_t = keep.tile([P, PACK], F32, name="gs_t")
         nc.sync.dma_start(out=gs_t[:], in_=gs.rearrange("(p t) o -> p (t o)", t=PACK))
-        n2_l = load_list("n2_l", n2)
-        n1_l = load_list("n1_l", n1)
         n3_l = load_list("n3_l", n3)
         cand_l = load_list("cand_l", cand)
         n4_l = load_list("n4_l", n4)
@@ -69,11 +70,9 @@ def tile_picked_dttzcksetepag_none_p_kernel(
             nc.sync.dma_start(out=sl_t[:], in_=sl.rearrange("(c p) o -> p (c o)", p=P))
             nc.sync.dma_start(out=th_t[:], in_=th.rearrange("(c p) o -> p (c o)", p=P))
 
-        xs = keep.tile([P, T], U8, name="xs")
-        nc.vector.memset(xs[:].bitcast(I32), 0)
-        for q in range(4):
-            rows = slice(32 * q, 32 * q + 4)
-            nc.vector.tensor_copy(out=xs[rows, :].bitcast(I32), in_=scale_rows[rows, :])
+        warm = keep.tile([P, 2], F32, name="warm")
+        nc.gpsimd.memset(warm[:, 0:1], 0.0)
+        nc.scalar.activation(warm[:, 1:2], warm[:, 0:1], ACT.Sigmoid)
 
         def quantize_weight(name, raw):
             grouped = keep.tile([P, PACK, P, PACK], BF16, name=name + "_grouped", align_bytes=64)
@@ -104,17 +103,16 @@ def tile_picked_dttzcksetepag_none_p_kernel(
         two_w = gather("two_w", U32, xw, two_l, S, tag="second_words")
 
         y_ps = [psum.tile([P, S], F32, name="y_ps%d" % t, tag="bank%d" % t) for t in range(PACK)]
-        for t in range(PACK):
+        operands = ((w1_c, w1_s, xq_w, xq_s), (w2_c, w2_s, two_w, two_s))
+        for t, g in ((0, 0), (1, 0), (0, 1), (1, 1), (2, 0), (2, 1), (3, 0), (3, 1)):
             cols = slice(t * P, (t + 1) * P)
-            nc.tensor.matmul_mx(out=y_ps[t][:], lhsT=w1_c[:, cols].bitcast(FP8X4), lhsT_scale=w1_s[:, cols],
-                                rhs=xq_w[:].bitcast(FP8X4), rhs_scale=xq_s[:], start=True, stop=False)
-        for t in range(PACK):
-            cols = slice(t * P, (t + 1) * P)
-            nc.tensor.matmul_mx(out=y_ps[t][:], lhsT=w2_c[:, cols].bitcast(FP8X4), lhsT_scale=w2_s[:, cols],
-                                rhs=two_w[:].bitcast(FP8X4), rhs_scale=two_s[:], start=False, stop=True)
+            w_c, w_s, x_w, x_s = operands[g]
+            nc.tensor.matmul_mx(out=y_ps[t][:], lhsT=w_c[:, cols].bitcast(FP8X4), lhsT_scale=w_s[:, cols],
+                                rhs=x_w[:].bitcast(FP8X4), rhs_scale=x_s[:], start=(g == 0), stop=(g == 1))
 
         ds = [keep.tile([P, S], F32, name="ds%d" % t) for t in range(PACK)]
-        for t in range(PACK):
+        nc.scalar.activation(ds[0][:], y_ps[0][:], ACT.Copy, scale=gs_t[:, 0:1])
+        for t in range(1, PACK):
             nc.vector.tensor_scalar(out=ds[t][:], in0=y_ps[t][:], scalar1=gs_t[:, t : t + 1], scalar2=None, op0=ALU.mult)
 
         cand_w = gather("cand_w", U32, xw, cand_l, C, tag="second_words")
@@ -122,36 +120,53 @@ def tile_picked_dttzcksetepag_none_p_kernel(
         bias = keep.tile([P, 4], F32, name="bias")
         nc.vector.scalar_tensor_tensor(out=bias[:], in0=sl_t[:], scalar=-1.0, in1=th_t[:], op0=ALU.mult, op1=ALU.mult)
 
-        far_head = keep.tile([P, PACK, HEAD], F32, name="far_head")
-        for pair in range(PACK // 2):
-            pa = keep.tile([P, 2, W], F32, name="pa%d" % pair, tag="pa%d" % pair)
-            for u in range(2):
-                nc.scalar.activation(pa[:, u, :], ds[2 * pair + u][:].indirect(n2_l[:]), ACT.Copy)
-            for u in range(2):
-                nc.scalar.activation(ds[2 * pair + u][:].indirect(n1_l[:]), pa[:, u, :], ACT.Copy)
-            for u in range(2):
-                t = 2 * pair + u
-                nc.scalar.activation(far_head[:, t, :], ds[t][:].indirect(entries(n3_l, 0, HEAD)), ACT.Copy)
-        far_rest = keep.tile([P, PACK, S - HEAD], F32, name="far_rest", tag="pa1")
-        for lo, hi in PIECES[1:]:
+        pa = [keep.tile([P, W], F32, name="pa%d" % t, tag="pa%d" % t) for t in range(PACK)]
+        far_a = keep.tile([P, PACK, QUARTER], F32, name="far_a")
+
+        def fetch_pa(t):
+            nc.scalar.activation(pa[t][:], ds[t][:].indirect(n2_l[:]), ACT.Copy)
+
+        def put_pa(t):
+            nc.scalar.activation(ds[t][:].indirect(n1_l[:]), pa[t][:], ACT.Copy)
+
+        def far_cols(far, t, lo, hi):
+            base = 0 if lo < QUARTER else QUARTER
+            return far[:, t, lo - base : hi - base]
+
+        def fetch_far(far, t, lo, hi):
+            nc.scalar.activation(far_cols(far, t, lo, hi), ds[t][:].indirect(entries(n3_l, lo, hi)), ACT.Copy)
+
+        fetch_pa(0)
+        fetch_pa(1)
+        put_pa(0)
+        put_pa(1)
+        fetch_pa(2)
+        fetch_pa(3)
+        fetch_far(far_a, 0, 0, QUARTER)
+        put_pa(2)
+        fetch_far(far_a, 1, 0, QUARTER)
+        put_pa(3)
+        fetch_far(far_a, 2, 0, QUARTER)
+        fetch_far(far_a, 3, 0, QUARTER)
+        far_b = keep.tile([P, PACK, S - QUARTER], F32, name="far_b", tag="pa3")
+        for lo, hi in ((QUARTER, HALF), (HALF, S)):
             for t in range(PACK):
-                nc.scalar.activation(far_rest[:, t, lo - HEAD : hi - HEAD], ds[t][:].indirect(entries(n3_l, lo, hi)), ACT.Copy)
+                fetch_far(far_b, t, lo, hi)
 
         z_codes = keep.tile([P, S], U32, name="z_codes", align_bytes=64)
         z_scales = keep.tile([P, S], U8, name="z_scales", align_bytes=64)
+        z_grouped = keep.tile([P, S, PACK], BF16, name="z_grouped", align_bytes=64)
 
-        def make_z(lo, hi):
-            n = hi - lo
-            planes = keep.tile([P, PACK, n], BF16, name="z_planes%d" % lo)
-            for t in range(PACK):
-                far = far_head[:, t, :] if lo == 0 else far_rest[:, t, lo - HEAD : hi - HEAD]
-                nc.vector.scalar_tensor_tensor(out=planes[:, t, :], in0=far, scalar=-0.5, in1=ds[t][:, lo:hi],
-                                               op0=ALU.mult, op1=ALU.add)
-            grouped = keep.tile([P, n, PACK], BF16, name="z_grouped%d" % lo, align_bytes=64)
-            nc.vector.tensor_copy(out=grouped[:].rearrange("p (c i) t -> p c t i", i=4),
-                                  in_=planes[:].rearrange("p t (c i) -> p c t i", i=4))
+        def form_z(dst, far, t, lo, hi):
+            nc.vector.scalar_tensor_tensor(out=dst, in0=far_cols(far, t, lo, hi), scalar=-0.5, in1=ds[t][:, lo:hi],
+                                           op0=ALU.mult, op1=ALU.add)
+
+        def form_z_in_place(t, lo, hi):
+            form_z(z_grouped[:, lo:hi, t], far_a if lo == 0 else far_b, t, lo, hi)
+
+        def quantize_z(lo, hi):
             nc.vector.quantize_mx(out=z_codes[:, lo:hi].bitcast(FP8X4), scales=z_scales[:, lo:hi],
-                                  in_=grouped[:].rearrange("p n t -> p (n t)"))
+                                  in_=z_grouped[:, lo:hi, :].rearrange("p n t -> p (n t)"))
 
         s = [keep.tile([P, S], F32, name="s%d" % c) for c in range(4)]
         page = [keep.tile([P, U], F32, name="page%d" % c) for c in range(4)]
@@ -163,23 +178,37 @@ def tile_picked_dttzcksetepag_none_p_kernel(
                                 rhs=z_codes[:, lo:hi].bitcast(FP8X4), rhs_scale=z_scales[:, lo:hi], start=True, stop=True)
             nc.vector.tensor_scalar(out=s[c][:, lo:hi], in0=acc[:], scalar1=0.0625, scalar2=None, op0=ALU.mult)
 
-        for i, (lo, hi) in enumerate(PIECES):
-            make_z(lo, hi)
-            for c in range(4):
-                score(c, lo, hi, 4 * ((i + 1) % 2) + c)
-        for lo, hi in PIECES[:-1]:
-            for c in range(4):
-                nc.scalar.activation(page[c][:].indirect(entries(n4_l, lo, hi)), s[c][:, lo:hi], ACT.Copy)
+        def put_s(c, lo, hi):
+            nc.scalar.activation(page[c][:].indirect(entries(n4_l, lo, hi)), s[c][:, lo:hi], ACT.Copy)
 
-        last = PIECES[-1][0]
+        for lo, hi in ((0, QUARTER), (QUARTER, HALF)):
+            for t in range(PACK):
+                form_z_in_place(t, lo, hi)
+            quantize_z(lo, hi)
+        early = ((0, 0, QUARTER), (1, 0, QUARTER), (0, QUARTER, HALF), (1, QUARTER, HALF), (2, 0, HALF), (3, 0, HALF))
+        for i, (c, lo, hi) in enumerate(early):
+            score(c, lo, hi, (4 + i) % 8)
+        for c, lo, hi in early:
+            put_s(c, lo, hi)
+
+        planes = keep.tile([P, PACK, HALF], BF16, name="z_planes")
+        for t in range(PACK):
+            form_z(planes[:, t, :], far_b, t, HALF, S)
+        nc.vector.tensor_copy(out=z_grouped[:, HALF:, :].rearrange("p (c i) t -> p c t i", i=4),
+                              in_=planes[:].rearrange("p t (c i) -> p c t i", i=4))
+        quantize_z(HALF, S)
+        for c in range(4):
+            score(c, HALF, S, 2 + c)
+
+        st = []
         for c in range(4):
             sg = keep.tile([P, S], F32, name="sg%d" % c)
-            for lo in range(0, S, S // 2):
-                hi = lo + S // 2
-                nc.scalar.activation(sg[:, lo:hi], s[c][:].indirect(entries(n6_l, lo, hi)), ACT.Sigmoid,
+            for lo in (0, HALF):
+                nc.scalar.activation(sg[:, lo : lo + HALF], s[c][:].indirect(entries(n6_l, lo, lo + HALF)), ACT.Sigmoid,
                                      bias=bias[:, c : c + 1], scale=sl_t[:, c : c + 1])
-            st = keep.tile([P, S], F32, name="st%d" % c)
-            nc.vector.tensor_tensor(out=st[:], in0=s[c][:], in1=sg[:], op=ALU.mult)
-            nc.scalar.activation(page[c][:].indirect(entries(n4_l, last, S)), s[c][:, last:], ACT.Copy)
-            nc.scalar.activation(page[c][:].indirect(n5_l[:]), st[:], ACT.Copy)
+            st.append(keep.tile([P, S], F32, name="st%d" % c))
+            nc.vector.tensor_tensor(out=st[c][:], in0=s[c][:], in1=sg[:], op=ALU.mult)
+            put_s(c, HALF, S)
+        for c in range(4):
+            nc.scalar.activation(page[c][:].indirect(n5_l[:]), st[c][:], ACT.Copy)
             nc.sync.dma_start(out=out[c * P : (c + 1) * P, :], in_=page[c][:])

@@ -40,9 +40,9 @@ def tile_picked_dttzcksetepag_none_p_kernel(
             nc.sync.dma_start(tile[:], src)
             return tile
 
-        def load_weight(name, src):
-            raw = keep.tile([P, PACK, H], F32, name=name)
-            nc.sync.dma_start(out=raw[:], in_=src.rearrange("(p j) c -> p j c", j=PACK))
+        def load_weight_half(name, src, h):
+            raw = keep.tile([P, PACK, H // 2], F32, name=name)
+            nc.sync.dma_start(out=raw[:], in_=src.rearrange("(p j) c -> p j c", j=PACK)[:, :, h * (H // 2) : (h + 1) * (H // 2)])
             return raw
 
         xs = keep.tile([P, T], U8, name="xs")
@@ -53,12 +53,20 @@ def tile_picked_dttzcksetepag_none_p_kernel(
         two_l = load_list("two_l", two)
         n2_l = load_list("n2_l", n2)
         n1_l = load_list("n1_l", n1)
-        w1_raw = load_weight("w1_raw", w1)
-        w2_raw = load_weight("w2_raw", w2)
+        raw = {}
+        raw[0, 0] = load_weight_half("w1_lo", w1, 0)
         xw = keep.tile([P, T], U32, name="xw")
         nc.sync.dma_start(out=xw[:].bitcast(I32), in_=x_words[0].rearrange("p n t -> p (n t)").bitcast(I32))
-        gs_t = keep.tile([P, PACK], F32, name="gs_t")
-        nc.sync.dma_start(out=gs_t[:], in_=gs.rearrange("(p t) o -> p (t o)", t=PACK))
+        raw[1, 0] = load_weight_half("w2_lo", w2, 0)
+        raw[0, 1] = load_weight_half("w1_hi", w1, 1)
+        raw[1, 1] = load_weight_half("w2_hi", w2, 1)
+        gs_t = keep.tile([P, 2], F32, name="gs_t")
+        gs_v = gs.rearrange("(h m t) o -> t m (h o)", h=2, t=PACK)
+        with nc.allow_non_contiguous_dma(reason="one value a partition and row tile"):
+            for u in range(2):
+                nc.gpsimd.dma_start(out=gs_t[u * 64 : (u + 1) * 64, 0:2], in_=gs_v[u])
+        gs_hi = keep.tile([P, 2], F32, name="gs_hi")
+        nc.gpsimd.dma_start(out=gs_hi[:], in_=gs.rearrange("(p t) o -> p (t o)", t=PACK)[:, 2:4])
         n3_l = load_list("n3_l", n3)
         cand_l = load_list("cand_l", cand)
         n4_l = load_list("n4_l", n4)
@@ -71,63 +79,97 @@ def tile_picked_dttzcksetepag_none_p_kernel(
             nc.sync.dma_start(out=th_t[:], in_=th.rearrange("(c p) o -> p (c o)", p=P))
 
         warm = keep.tile([P, 2], F32, name="warm")
-        nc.gpsimd.memset(warm[:, 0:1], 0.0)
+        nc.vector.memset(warm[:, 0:1], 0.0)
         nc.scalar.activation(warm[:, 1:2], warm[:, 0:1], ACT.Sigmoid)
 
-        def quantize_weight(name, raw):
-            grouped = keep.tile([P, PACK, P, PACK], BF16, name=name + "_grouped", align_bytes=64)
-            dst = grouped[:].rearrange("p t m j -> p m j t")
-            src = raw[:].rearrange("p j (m t) -> p m j t", t=PACK)
-            nc.vector.tensor_copy(out=dst[:, : P // 2], in_=src[:, : P // 2])
-            nc.scalar.copy(out=dst[:, P // 2 :], in_=src[:, P // 2 :])
-            return grouped
+        w_codes = [keep.tile([P, H], U32, name="w%d_codes" % g, align_bytes=64) for g in range(2)]
+        w_scales = [keep.tile([P, H], U8, name="w%d_scales" % g, align_bytes=64) for g in range(2)]
+        grouped = {}
 
-        def quantize(name, grouped, width):
-            codes = keep.tile([P, width], U32, name=name + "_codes", align_bytes=64)
-            scales = keep.tile([P, width], U8, name=name + "_scales", align_bytes=64)
-            nc.vector.quantize_mx(out=codes[:].bitcast(FP8X4), scales=scales[:], in_=grouped)
-            return codes, scales
+        def round_weight(engine, g, h, t_lo, t_hi):
+            tile = keep.tile([P, t_hi - t_lo, 64, PACK], BF16, name="w_grouped%d%d%d" % (g, h, t_lo), align_bytes=64)
+            dst = tile[:].rearrange("p t m j -> p m j t")
+            src = raw[g, h][:].rearrange("p j (m t) -> p m j t", t=PACK)[:, :, :, t_lo:t_hi]
+            if engine == "vector":
+                nc.vector.tensor_copy(out=dst, in_=src)
+            else:
+                nc.scalar.copy(out=dst, in_=src)
+            for t in range(t_lo, t_hi):
+                grouped[g, h, t] = (tile, t - t_lo)
+
+        def quantize_weight(g, h, t, count):
+            tile, at = grouped[g, h, t]
+            lo = h * P if t == 0 else t * P + h * 64
+            cols = slice(lo, lo + 64 * count)
+            nc.vector.quantize_mx(out=w_codes[g][:, cols].bitcast(FP8X4), scales=w_scales[g][:, cols],
+                                  in_=tile[:, at : at + count].rearrange("p t m j -> p (t m j)"))
 
         def gather(name, dtype, window, lst, n, tag=None):
             got = keep.tile([P, n], dtype, name=name, tag=tag or name, align_bytes=64)
             nc.vector.tensor_copy(out=got[:], in_=window[:].indirect(lst[:]))
             return got
 
-        w1_g = quantize_weight("w1", w1_raw)
-        xq_s = gather("xq_s", U8, xs, offs_l, S)
-        w1_c, w1_s = quantize("w1", w1_g[:].rearrange("p t m j -> p (t m j)"), H)
-        two_s = gather("two_s", U8, xs, two_l, S)
-        w2_g = quantize_weight("w2", w2_raw)
-        w2_c, w2_s = quantize("w2", w2_g[:].rearrange("p t m j -> p (t m j)"), H)
-        xq_w = gather("xq_w", U32, xw, offs_l, S, tag="first_words")
-        two_w = gather("two_w", U32, xw, two_l, S, tag="second_words")
-
         y_ps = [psum.tile([P, S], F32, name="y_ps%d" % t, tag="bank%d" % t) for t in range(PACK)]
-        operands = ((w1_c, w1_s, xq_w, xq_s), (w2_c, w2_s, two_w, two_s))
-        for t, g in ((0, 0), (1, 0), (0, 1), (1, 1), (2, 0), (2, 1), (3, 0), (3, 1)):
+        rows_of = [keep.tile([P, S], F32, name="rows%d" % t, tag="rows%d" % t) for t in range(PACK)]
+
+        def project(t, g):
             cols = slice(t * P, (t + 1) * P)
-            w_c, w_s, x_w, x_s = operands[g]
-            nc.tensor.matmul_mx(out=y_ps[t][:], lhsT=w_c[:, cols].bitcast(FP8X4), lhsT_scale=w_s[:, cols],
+            x_w, x_s = picked[g]
+            nc.tensor.matmul_mx(out=y_ps[t][:], lhsT=w_codes[g][:, cols].bitcast(FP8X4), lhsT_scale=w_scales[g][:, cols],
                                 rhs=x_w[:].bitcast(FP8X4), rhs_scale=x_s[:], start=(g == 0), stop=(g == 1))
 
-        ds = [keep.tile([P, S], F32, name="ds%d" % t) for t in range(PACK)]
-        nc.scalar.activation(ds[0][:], y_ps[0][:], ACT.Copy, scale=gs_t[:, 0:1])
-        for t in range(1, PACK):
-            nc.vector.tensor_scalar(out=ds[t][:], in0=y_ps[t][:], scalar1=gs_t[:, t : t + 1], scalar2=None, op0=ALU.mult)
+        def leave_psum(t):
+            gain = gs_t[:, t : t + 1] if t < 2 else gs_hi[:, t - 2 : t - 1]
+            nc.vector.tensor_scalar(out=rows_of[t][:], in0=y_ps[t][:], scalar1=gain, scalar2=None, op0=ALU.mult)
+
+        pa = [keep.tile([P, W], F32, name="pa%d" % t) for t in range(PACK)]
+
+        def fetch_pa(t):
+            nc.scalar.activation(pa[t][:], rows_of[t][:].indirect(n2_l[:]), ACT.Copy)
+
+        def put_pa(t):
+            nc.scalar.activation(rows_of[t][:].indirect(n1_l[:]), pa[t][:], ACT.Copy)
+
+        round_weight("scalar", 0, 0, 0, 4)
+        xq_s = gather("xq_s", U8, xs, offs_l, S)
+        two_s = gather("two_s", U8, xs, two_l, S)
+        quantize_weight(0, 0, 0, 2)
+        quantize_weight(0, 0, 2, 1)
+        quantize_weight(0, 0, 3, 1)
+        xq_w = gather("xq_w", U32, xw, offs_l, S, tag="first_words")
+        two_w = gather("two_w", U32, xw, two_l, S, tag="second_words")
+        picked = ((xq_w, xq_s), (two_w, two_s))
+        project(0, 0)
+        round_weight("vector", 1, 0, 0, 2)
+        round_weight("scalar", 1, 0, 2, 4)
+        quantize_weight(1, 0, 0, 2)
+        project(0, 1)
+        leave_psum(0)
+        round_weight("scalar", 0, 1, 0, 2)
+        round_weight("scalar", 0, 1, 2, 4)
+        quantize_weight(0, 1, 0, 2)
+        project(1, 0)
+        round_weight("vector", 1, 1, 0, 2)
+        quantize_weight(1, 1, 0, 2)
+        project(1, 1)
+        fetch_pa(0)
+        round_weight("scalar", 1, 1, 2, 4)
+        put_pa(0)
+        leave_psum(1)
+        for t in (2, 3):
+            quantize_weight(1, 0, t, 1)
+            quantize_weight(0, 1, t, 1)
+            quantize_weight(1, 1, t, 1)
+            project(t, 0)
+            project(t, 1)
+            leave_psum(t)
 
         cand_w = gather("cand_w", U32, xw, cand_l, C, tag="second_words")
         cand_s = gather("cand_s", U8, xs, cand_l, C, tag="first_words")
         bias = keep.tile([P, 4], F32, name="bias")
         nc.vector.scalar_tensor_tensor(out=bias[:], in0=sl_t[:], scalar=-1.0, in1=th_t[:], op0=ALU.mult, op1=ALU.mult)
 
-        pa = [keep.tile([P, W], F32, name="pa%d" % t, tag="pa%d" % t) for t in range(PACK)]
         far_a = keep.tile([P, PACK, QUARTER], F32, name="far_a")
-
-        def fetch_pa(t):
-            nc.scalar.activation(pa[t][:], ds[t][:].indirect(n2_l[:]), ACT.Copy)
-
-        def put_pa(t):
-            nc.scalar.activation(ds[t][:].indirect(n1_l[:]), pa[t][:], ACT.Copy)
 
         def far_cols(far, t, lo, hi):
             base = 0 if lo < QUARTER else QUARTER
@@ -136,19 +178,20 @@ def tile_picked_dttzcksetepag_none_p_kernel(
         def fetch_far(far, t, lo, hi):
             nc.scalar.activation(far_cols(far, t, lo, hi), ds[t][:].indirect(entries(n3_l, lo, hi)), ACT.Copy)
 
-        fetch_pa(0)
+        slot1 = keep.tile([P, S], F32, name="slot1")
+        ds = [rows_of[0], slot1, rows_of[2], rows_of[3]]
+        nc.sync.dma_start(out=slot1[0:64, :], in_=rows_of[0][64:128, :])
         fetch_pa(1)
-        put_pa(0)
-        put_pa(1)
         fetch_pa(2)
+        put_pa(1)
+        nc.sync.dma_start(out=rows_of[0][64:128, :], in_=rows_of[1][0:64, :])
+        nc.vector.tensor_copy(out=slot1[64:128, :], in_=rows_of[1][64:128, :])
         fetch_pa(3)
-        fetch_far(far_a, 0, 0, QUARTER)
         put_pa(2)
-        fetch_far(far_a, 1, 0, QUARTER)
         put_pa(3)
-        fetch_far(far_a, 2, 0, QUARTER)
-        fetch_far(far_a, 3, 0, QUARTER)
-        far_b = keep.tile([P, PACK, S - QUARTER], F32, name="far_b", tag="pa3")
+        for t in (2, 1, 3, 0):
+            fetch_far(far_a, t, 0, QUARTER)
+        far_b = keep.tile([P, PACK, S - QUARTER], F32, name="far_b", tag="rows1")
         for lo, hi in ((QUARTER, HALF), (HALF, S)):
             for t in range(PACK):
                 fetch_far(far_b, t, lo, hi)
@@ -182,7 +225,7 @@ def tile_picked_dttzcksetepag_none_p_kernel(
             nc.scalar.activation(page[c][:].indirect(entries(n4_l, lo, hi)), s[c][:, lo:hi], ACT.Copy)
 
         for lo, hi in ((0, QUARTER), (QUARTER, HALF)):
-            for t in range(PACK):
+            for t in (2, 1, 3, 0) if lo == 0 else range(PACK):
                 form_z_in_place(t, lo, hi)
             quantize_z(lo, hi)
         early = ((0, 0, QUARTER), (1, 0, QUARTER), (0, QUARTER, HALF), (1, QUARTER, HALF), (2, 0, HALF), (3, 0, HALF))

from contextlib import ExitStack

import concourse.mybir as mybir

F32 = mybir.dt.float32
BF16 = mybir.dt.bfloat16
I32 = mybir.dt.int32
U32 = mybir.dt.uint32
U16 = mybir.dt.uint16
U8 = mybir.dt.uint8
FP8X4 = mybir.dt.float8_e4m3fn_x4
ACT = mybir.ActivationFunctionType
ALU = mybir.AluOpType

P = 128
PACK = 4
K, T, S, H, W, C, U = 512, 2048, 256, 512, 128, 512, 512
LANES = 16
HALF = S // 2
QUARTER = S // 4

FLOPS = 2 * K * H * S * 2 + 2 * H * C * S


def entries(lst, lo, hi):
    return lst[:, lo // LANES : hi // LANES]


def tile_picked_dttzcksetepag_none_p_kernel(
    tc, x_words, x_scales, w1, w2, gs, sl, th, offs, two, n1, n2, n3, cand, n4, n5, n6, out
):
    nc = tc.nc
    with ExitStack() as ctx:
        lists = ctx.enter_context(tc.tile_pool(name="lists", bufs=1))
        keep = ctx.enter_context(tc.tile_pool(name="keep", bufs=1))
        psum = ctx.enter_context(tc.psum_pool(name="psum", bufs=1))

        def load_list(name, src):
            tile = lists.tile(list(src.shape), U16, name=name)
            nc.sync.dma_start(tile[:], src)
            return tile

        def load_weight_half(name, src, h):
            raw = keep.tile([P, PACK, H // 2], F32, name=name)
            nc.sync.dma_start(out=raw[:], in_=src.rearrange("(p j) c -> p j c", j=PACK)[:, :, h * (H // 2) : (h + 1) * (H // 2)])
            return raw

        xs = keep.tile([P, T], U8, name="xs")
        nc.vector.memset(xs[:].bitcast(I32), 0)
        for q in range(4):
            nc.scalar.dma_start(out=xs[32 * q : 32 * q + 4, :].bitcast(I32), in_=x_scales[0][4 * q : 4 * q + 4, :].bitcast(I32))
        offs_l = load_list("offs_l", offs)
        two_l = load_list("two_l", two)
        n2_l = load_list("n2_l", n2)
        n1_l = load_list("n1_l", n1)
        raw = {}
        raw[0, 0] = load_weight_half("w1_lo", w1, 0)
        xw = keep.tile([P, T], U32, name="xw")
        nc.sync.dma_start(out=xw[:].bitcast(I32), in_=x_words[0].rearrange("p n t -> p (n t)").bitcast(I32))
        raw[1, 0] = load_weight_half("w2_lo", w2, 0)
        raw[0, 1] = load_weight_half("w1_hi", w1, 1)
        raw[1, 1] = load_weight_half("w2_hi", w2, 1)
        gs_t = keep.tile([P, 2], F32, name="gs_t")
        gs_v = gs.rearrange("(h m t) o -> t m (h o)", h=2, t=PACK)
        with nc.allow_non_contiguous_dma(reason="one value a partition and row tile"):
            for u in range(2):
                nc.gpsimd.dma_start(out=gs_t[u * 64 : (u + 1) * 64, 0:2], in_=gs_v[u])
        gs_hi = keep.tile([P, 2], F32, name="gs_hi")
        nc.gpsimd.dma_start(out=gs_hi[:], in_=gs.rearrange("(p t) o -> p (t o)", t=PACK)[:, 2:4])
        n3_l = load_list("n3_l", n3)
        cand_l = load_list("cand_l", cand)
        n4_l = load_list("n4_l", n4)
        n6_l = load_list("n6_l", n6)
        n5_l = load_list("n5_l", n5)
        sl_t = keep.tile([P, 4], F32, name="sl_t")
        th_t = keep.tile([P, 4], F32, name="th_t")
        with nc.allow_non_contiguous_dma(reason="one value a partition and row tile"):
            nc.sync.dma_start(out=sl_t[:], in_=sl.rearrange("(c p) o -> p (c o)", p=P))
            nc.sync.dma_start(out=th_t[:], in_=th.rearrange("(c p) o -> p (c o)", p=P))

        warm = keep.tile([P, 2], F32, name="warm")
        nc.vector.memset(warm[:, 0:1], 0.0)
        nc.scalar.activation(warm[:, 1:2], warm[:, 0:1], ACT.Sigmoid)

        w_codes = [keep.tile([P, H], U32, name="w%d_codes" % g, align_bytes=64) for g in range(2)]
        w_scales = [keep.tile([P, H], U8, name="w%d_scales" % g, align_bytes=64) for g in range(2)]
        grouped = {}

        def round_weight(engine, g, h, t_lo, t_hi):
            tile = keep.tile([P, t_hi - t_lo, 64, PACK], BF16, name="w_grouped%d%d%d" % (g, h, t_lo), align_bytes=64)
            dst = tile[:].rearrange("p t m j -> p m j t")
            src = raw[g, h][:].rearrange("p j (m t) -> p m j t", t=PACK)[:, :, :, t_lo:t_hi]
            if engine == "vector":
                nc.vector.tensor_copy(out=dst, in_=src)
            else:
                nc.scalar.copy(out=dst, in_=src)
            for t in range(t_lo, t_hi):
                grouped[g, h, t] = (tile, t - t_lo)

        def quantize_weight(g, h, t, count):
            tile, at = grouped[g, h, t]
            lo = h * P if t == 0 else t * P + h * 64
            cols = slice(lo, lo + 64 * count)
            nc.vector.quantize_mx(out=w_codes[g][:, cols].bitcast(FP8X4), scales=w_scales[g][:, cols],
                                  in_=tile[:, at : at + count].rearrange("p t m j -> p (t m j)"))

        def gather(name, dtype, window, lst, n, tag=None):
            got = keep.tile([P, n], dtype, name=name, tag=tag or name, align_bytes=64)
            nc.vector.tensor_copy(out=got[:], in_=window[:].indirect(lst[:]))
            return got

        y_ps = [psum.tile([P, S], F32, name="y_ps%d" % t, tag="bank%d" % t) for t in range(PACK)]
        rows_of = [keep.tile([P, S], F32, name="rows%d" % t, tag="rows%d" % t) for t in range(PACK)]

        def project(t, g):
            cols = slice(t * P, (t + 1) * P)
            x_w, x_s = picked[g]
            nc.tensor.matmul_mx(out=y_ps[t][:], lhsT=w_codes[g][:, cols].bitcast(FP8X4), lhsT_scale=w_scales[g][:, cols],
                                rhs=x_w[:].bitcast(FP8X4), rhs_scale=x_s[:], start=(g == 0), stop=(g == 1))

        def leave_psum(t):
            gain = gs_t[:, t : t + 1] if t < 2 else gs_hi[:, t - 2 : t - 1]
            nc.vector.tensor_scalar(out=rows_of[t][:], in0=y_ps[t][:], scalar1=gain, scalar2=None, op0=ALU.mult)

        pa = [keep.tile([P, W], F32, name="pa%d" % t) for t in range(PACK)]

        def fetch_pa(t):
            nc.scalar.activation(pa[t][:], rows_of[t][:].indirect(n2_l[:]), ACT.Copy)

        def put_pa(t):
            nc.scalar.activation(rows_of[t][:].indirect(n1_l[:]), pa[t][:], ACT.Copy)

        round_weight("scalar", 0, 0, 0, 4)
        xq_s = gather("xq_s", U8, xs, offs_l, S)
        two_s = gather("two_s", U8, xs, two_l, S)
        quantize_weight(0, 0, 0, 2)
        quantize_weight(0, 0, 2, 1)
        quantize_weight(0, 0, 3, 1)
        xq_w = gather("xq_w", U32, xw, offs_l, S, tag="first_words")
        two_w = gather("two_w", U32, xw, two_l, S, tag="second_words")
        picked = ((xq_w, xq_s), (two_w, two_s))
        project(0, 0)
        round_weight("vector", 1, 0, 0, 2)
        round_weight("scalar", 1, 0, 2, 4)
        quantize_weight(1, 0, 0, 2)
        project(0, 1)
        leave_psum(0)
        round_weight("scalar", 0, 1, 0, 2)
        round_weight("scalar", 0, 1, 2, 4)
        quantize_weight(0, 1, 0, 2)
        project(1, 0)
        round_weight("vector", 1, 1, 0, 2)
        quantize_weight(1, 1, 0, 2)
        project(1, 1)
        fetch_pa(0)
        round_weight("scalar", 1, 1, 2, 4)
        put_pa(0)
        leave_psum(1)
        for t in (2, 3):
            quantize_weight(1, 0, t, 1)
            quantize_weight(0, 1, t, 1)
            quantize_weight(1, 1, t, 1)
            project(t, 0)
            project(t, 1)
            leave_psum(t)

        cand_w = gather("cand_w", U32, xw, cand_l, C, tag="second_words")
        cand_s = gather("cand_s", U8, xs, cand_l, C, tag="first_words")
        bias = keep.tile([P, 4], F32, name="bias")
        nc.vector.scalar_tensor_tensor(out=bias[:], in0=sl_t[:], scalar=-1.0, in1=th_t[:], op0=ALU.mult, op1=ALU.mult)

        far_a = keep.tile([P, PACK, QUARTER], F32, name="far_a")

        def far_cols(far, t, lo, hi):
            base = 0 if lo < QUARTER else QUARTER
            return far[:, t, lo - base : hi - base]

        def fetch_far(far, t, lo, hi):
            nc.scalar.activation(far_cols(far, t, lo, hi), ds[t][:].indirect(entries(n3_l, lo, hi)), ACT.Copy)

        slot1 = keep.tile([P, S], F32, name="slot1")
        ds = [rows_of[0], slot1, rows_of[2], rows_of[3]]
        nc.sync.dma_start(out=slot1[0:64, :], in_=rows_of[0][64:128, :])
        fetch_pa(1)
        fetch_pa(2)
        put_pa(1)
        nc.sync.dma_start(out=rows_of[0][64:128, :], in_=rows_of[1][0:64, :])
        nc.vector.tensor_copy(out=slot1[64:128, :], in_=rows_of[1][64:128, :])
        fetch_pa(3)
        put_pa(2)
        put_pa(3)
        for t in (2, 1, 3, 0):
            fetch_far(far_a, t, 0, QUARTER)
        far_b = keep.tile([P, PACK, S - QUARTER], F32, name="far_b", tag="rows1")
        for lo, hi in ((QUARTER, HALF), (HALF, S)):
            for t in range(PACK):
                fetch_far(far_b, t, lo, hi)

        z_codes = keep.tile([P, S], U32, name="z_codes", align_bytes=64)
        z_scales = keep.tile([P, S], U8, name="z_scales", align_bytes=64)
        z_grouped = keep.tile([P, S, PACK], BF16, name="z_grouped", align_bytes=64)

        def form_z(dst, far, t, lo, hi):
            nc.vector.scalar_tensor_tensor(out=dst, in0=far_cols(far, t, lo, hi), scalar=-0.5, in1=ds[t][:, lo:hi],
                                           op0=ALU.mult, op1=ALU.add)

        def form_z_in_place(t, lo, hi):
            form_z(z_grouped[:, lo:hi, t], far_a if lo == 0 else far_b, t, lo, hi)

        def quantize_z(lo, hi):
            nc.vector.quantize_mx(out=z_codes[:, lo:hi].bitcast(FP8X4), scales=z_scales[:, lo:hi],
                                  in_=z_grouped[:, lo:hi, :].rearrange("p n t -> p (n t)"))

        s = [keep.tile([P, S], F32, name="s%d" % c) for c in range(4)]
        page = [keep.tile([P, U], F32, name="page%d" % c) for c in range(4)]

        def score(c, lo, hi, bank):
            acc = psum.tile([P, hi - lo], F32, name="s_ps%d_%d" % (c, lo), tag="bank%d" % bank)
            rows = slice(c * P, (c + 1) * P)
            nc.tensor.matmul_mx(out=acc[:], lhsT=cand_w[:, rows].bitcast(FP8X4), lhsT_scale=cand_s[:, rows],
                                rhs=z_codes[:, lo:hi].bitcast(FP8X4), rhs_scale=z_scales[:, lo:hi], start=True, stop=True)
            nc.vector.tensor_scalar(out=s[c][:, lo:hi], in0=acc[:], scalar1=0.0625, scalar2=None, op0=ALU.mult)

        def put_s(c, lo, hi):
            nc.scalar.activation(page[c][:].indirect(entries(n4_l, lo, hi)), s[c][:, lo:hi], ACT.Copy)

        for lo, hi in ((0, QUARTER), (QUARTER, HALF)):
            for t in (2, 1, 3, 0) if lo == 0 else range(PACK):
                form_z_in_place(t, lo, hi)
            quantize_z(lo, hi)
        early = ((0, 0, QUARTER), (1, 0, QUARTER), (0, QUARTER, HALF), (1, QUARTER, HALF), (2, 0, HALF), (3, 0, HALF))
        for i, (c, lo, hi) in enumerate(early):
            score(c, lo, hi, (4 + i) % 8)
        for c, lo, hi in early:
            put_s(c, lo, hi)

        planes = keep.tile([P, PACK, HALF], BF16, name="z_planes")
        for t in range(PACK):
            form_z(planes[:, t, :], far_b, t, HALF, S)
        nc.vector.tensor_copy(out=z_grouped[:, HALF:, :].rearrange("p (c i) t -> p c t i", i=4),
                              in_=planes[:].rearrange("p t (c i) -> p c t i", i=4))
        quantize_z(HALF, S)
        for c in range(4):
            score(c, HALF, S, 2 + c)

        st = []
        for c in range(4):
            sg = keep.tile([P, S], F32, name="sg%d" % c)
            for lo in (0, HALF):
                nc.scalar.activation(sg[:, lo : lo + HALF], s[c][:].indirect(entries(n6_l, lo, lo + HALF)), ACT.Sigmoid,
                                     bias=bias[:, c : c + 1], scale=sl_t[:, c : c + 1])
            st.append(keep.tile([P, S], F32, name="st%d" % c))
            nc.vector.tensor_tensor(out=st[c][:], in0=s[c][:], in1=sg[:], op=ALU.mult)
            put_s(c, HALF, S)
        for c in range(4):
            nc.scalar.activation(page[c][:].indirect(n5_l[:]), st[c][:], ACT.Copy)
            nc.sync.dma_start(out=out[c * P : (c + 1) * P, :], in_=page[c][:])
